import numpy as np
import ml_dtypes


def mxq(x, axis, fmt="e4m3"):
    dtype, down = {"e4m3": (ml_dtypes.float8_e4m3fn, 7), "e5m2": (ml_dtypes.float8_e5m2, 14)}[fmt]
    v = np.moveaxis(np.asarray(x, np.float32).astype(ml_dtypes.bfloat16).astype(np.float64), axis, -1)
    blocks = v.reshape(v.shape[:-1] + (-1, 32))
    amax = np.abs(blocks).max(-1, keepdims=True)
    byte = np.maximum(np.where(amax > 0, np.frexp(amax)[1] - 1 + 127, 0) - down, 1)
    scale = np.exp2(byte - 127.0)
    codes = (blocks / scale).astype(np.float32).astype(dtype).astype(np.float64)
    return np.moveaxis((codes * scale).reshape(v.shape), -1, axis)


WIDE = False


def mx_kscale(k):
    if not WIDE:
        return np.ones(k)
    levels = np.array([10, -10, 5, -5, 0])
    if k % 512:
        return np.exp2(np.random.permutation(np.resize(levels, k // 32))).repeat(32)
    a = np.empty((k // 512, 16))
    for p in range(k // 512):
        a[p, :8] = np.random.permutation(np.resize(levels, 8))
        for g in range(8):
            far = levels[np.abs(levels - a[p, g]) >= 10]
            a[p, g + 8] = far[np.random.randint(len(far))]
    return np.exp2(a.ravel()).repeat(32)


def f64(x):
    return np.asarray(x).astype(np.float64)


def striped(idx):
    return np.tile(idx.reshape(-1, 16).T, (8, 1)).astype(np.uint16)


def unstriped(offs):
    return offs[:16].T.reshape(-1).astype(np.int64)


def striped8(idx):
    return np.concatenate([x.reshape(-1, 16).T for x in idx]).astype(np.uint16)


def runs(offs, k):
    lists = np.stack([offs[16 * r : 16 * r + 16].T.reshape(-1) for r in range(8)]).astype(np.int64)
    return lists[np.arange(k) % 512 // 64]


def pack_weight(w):
    k, n = w.shape
    w = f64(np.asarray(w, np.float32).astype(ml_dtypes.bfloat16)).reshape(k // 32, 32, n)
    amax = np.abs(w).max(1)
    byte = np.clip(np.where(amax > 0, np.frexp(amax)[1] - 1 + 127 - 7, 1), 1, 254)
    scaled = (w * np.exp2(127.0 - byte)[:, None, :]).reshape(k, n).astype(np.float32)
    words = np.ascontiguousarray(scaled.reshape(k // 512, 128, 4, n).transpose(0, 1, 3, 2)).astype(ml_dtypes.float8_e4m3fn).view(np.uint8)
    return words, np.ascontiguousarray(byte.astype(np.uint8).reshape(k // 512, 16, n))


def unpack_weight(words, scales):
    g, p, n, _ = words.shape
    vals = np.ascontiguousarray(words).view(ml_dtypes.float8_e4m3fn).astype(np.float64) * np.repeat(np.exp2(scales.astype(np.float64) - 127.0), 8, axis=1)[..., None]
    return vals.transpose(0, 1, 3, 2).reshape(g * 512, n)


def relu(v):
    return np.maximum(v, 0.0)


def sigmoid(v):
    return 1.0 / (1.0 + np.exp(-np.maximum(v, -700.0)))

def planes(y):
    n, m = y.shape
    v = y.astype(np.float32).astype(ml_dtypes.bfloat16).astype(np.float64).reshape(n // 32, 32, m)
    top = np.abs(v).max(1)
    byte = np.clip(np.where(top > 0, np.frexp(top)[1] - 1 + 127 - 7, 1), 1, 254)
    codes = (v * np.exp2(127.0 - byte)[:, None, :]).reshape(n, m).astype(np.float32).astype(ml_dtypes.float8_e4m3fn).view(np.uint8)
    words = codes.reshape(n // 512, 128, 4, m).transpose(0, 1, 3, 2)
    return np.ascontiguousarray(words), np.ascontiguousarray(byte.astype(np.uint8).reshape(n // 512, 16, m))


K, T, S, N, H = 512, 2048, 512, 512, 512


def setup_inputs():
    n = np.random.standard_normal
    s = mx_kscale(K)[:, None]
    u = mx_kscale(H)
    packed_xT = pack_weight(n((K, T)) * s)
    packed_w1 = pack_weight(n((K, H)) / np.sqrt(K) / s)
    packed_w2 = pack_weight(n((H, N)) / np.sqrt(H) / u[:, None])
    return {
        "x_words": packed_xT[0],
        "x_scales": packed_xT[1],
        "w1_words": packed_w1[0],
        "w1_scales": packed_w1[1],
        "gn": (np.random.uniform(0.5, 1.5, (H, 1)) * u[:, None]).astype(np.float32),
        "w2_words": packed_w2[0],
        "w2_scales": packed_w2[1],
        "offs": striped(np.random.permutation(T)[:S]),
        "c1": striped8(np.stack([np.random.permutation(S) for _ in range(8)])),
        "c2": striped8(np.stack([np.random.permutation(S) for _ in range(8)])),
        "c3": striped8(np.stack([np.random.permutation(S) for _ in range(8)])),
    }


def reference(x_words, x_scales, w1_words, w1_scales, gn, w2_words, w2_scales, offs, c1, c2, c3):
    xq = unpack_weight(x_words, x_scales)[:, unstriped(offs)]
    p = sigmoid(2.0 * ((unpack_weight(w1_words, w1_scales).T @ xq)))
    a = p[np.arange(H)[:, None], runs(c1, H)]
    c = p[np.arange(H)[:, None], runs(c3, H)]
    b = p[np.arange(H)[:, None], runs(c2, H)]
    im = np.clip(b - a + 1, 0.0, 1.0)
    z = f64(gn) * (np.maximum(relu(a + c + -1), im + -0.5))
    out_0 = unpack_weight(w2_words, w2_scales).T @ mxq(z, 0, "e4m3")
    return (out_0,) + planes(out_0)

@@ -1,0 +1,215 @@
+from contextlib import ExitStack
+
+import concourse.mybir as mybir
+
+K, T, S, H, N = 512, 2048, 512, 512, 512
+FLOPS = 2 * K * H * S + 2 * H * N * S
+
+F32 = mybir.dt.float32
+BF16 = mybir.dt.bfloat16
+I32 = mybir.dt.int32
+U32 = mybir.dt.uint32
+U16 = mybir.dt.uint16
+U8 = mybir.dt.uint8
+FP8X4 = mybir.dt.float8_e4m3fn_x4
+ALU = mybir.AluOpType
+ACT = mybir.ActivationFunctionType
+
+P = 128
+PACK = 4
+QUADS = 4
+BLOCK = 128
+CHUNKS = ((0, 256), (256, 128), (384, 128))
+W1_ROW, W2_ROW = 4, 8
+
+
+def tile_picked_lukaslog_none_po_kernel(
+    tc, x_words, x_scales, w1_words, w1_scales, gn, w2_words, w2_scales, offs, c1, c2, c3, out_0, out_1, out_2
+):
+    nc = tc.nc
+
+    def as_words(dram):
+        return dram[0].rearrange("p n t -> p (n t)").bitcast(I32)
+
+    def load_scale_rows(queue, tile, dram, first_row, q):
+        rows = slice(32 * q + first_row, 32 * q + first_row + 4)
+        queue.dma_start(out=tile[rows, :].bitcast(I32), in_=dram[0, 4 * q : 4 * q + 4, :].bitcast(I32))
+
+    def deal(dealt, raw):
+        nc.vector.tensor_copy(
+            out=dealt.rearrange("p (t m) -> p t m", t=PACK), in_=raw.rearrange("p (m t) -> p t m", t=PACK)
+        )
+
+    with ExitStack() as ctx:
+        lists = ctx.enter_context(tc.tile_pool(name="lists", bufs=1))
+        keep = ctx.enter_context(tc.tile_pool(name="keep", bufs=1))
+        psum = ctx.enter_context(tc.psum_pool(name="psum", bufs=1))
+
+        offs_sb = lists.tile([P, S // 16], U16)
+        c1_sb = lists.tile([P, S // 16], U16)
+        c2_sb = lists.tile([P, S // 16], U16)
+        c3_sb = lists.tile([P, S // 16], U16)
+
+        xw = keep.tile([P, T], U32, align_bytes=64)
+        xs = keep.tile([P, T], U8, align_bytes=64)
+        w1w = keep.tile([P, H], U32, align_bytes=64)
+        w1s = keep.tile([P, H], U8, align_bytes=64)
+        w2w = keep.tile([P, N], U32, align_bytes=64)
+        w2s = keep.tile([P, N], U8, align_bytes=64)
+        gain = keep.tile([P, PACK], F32, align_bytes=64)
+        warm = keep.tile([P, 2], F32, align_bytes=64)
+
+        nc.vector.memset(xs[:].bitcast(I32), 0)
+        nc.gpsimd.memset(w1s[:].bitcast(I32), 0)
+        nc.vector.memset(w2s[:].bitcast(I32), 0)
+        nc.vector.memset(warm[:, 0:1], 0.0)
+        nc.scalar.activation(warm[:, 1:2], warm[:, 0:1], ACT.Sigmoid)
+
+        nc.sync.dma_start(offs_sb[:], offs)
+        nc.sync.dma_start(out=w1w[:].bitcast(I32), in_=as_words(w1_words))
+        nc.sync.dma_start(out=xw[:].bitcast(I32), in_=as_words(x_words))
+        for q in range(QUADS):
+            load_scale_rows(nc.sync, xs, x_scales, 0, q)
+        for q in range(QUADS):
+            load_scale_rows(nc.gpsimd if q == 3 else nc.sync, w1s, w1_scales, W1_ROW, q)
+        nc.sync.dma_start(c1_sb[:], c1)
+        nc.sync.dma_start(c3_sb[:], c3)
+        nc.sync.dma_start(c2_sb[:], c2)
+        nc.sync.dma_start(out=gain[:], in_=gn.rearrange("(p t) o -> p (t o)", t=PACK))
+        nc.sync.dma_start(out=w2w[:].bitcast(I32), in_=as_words(w2_words))
+        for q in range(QUADS):
+            load_scale_rows(nc.sync, w2s, w2_scales, W2_ROW, q)
+
+        w1w_d = keep.tile([P, H], U32, align_bytes=64)
+        w1s_d = keep.tile([P, H], U8, align_bytes=64)
+        w2w_d = keep.tile([P, N], U32, align_bytes=64)
+        w2s_d = keep.tile([P, N], U8, align_bytes=64)
+        gw = keep.tile([P, S], U32, align_bytes=64)
+        gs = keep.tile([P, S], U8, align_bytes=64)
+
+        deal(w1w_d[:].bitcast(I32), w1w[:].bitcast(I32))
+        nc.vector.tensor_copy(gs[:], xs[:].indirect(offs_sb[:]))
+        half = S // 2
+        for i in range(2):
+            nc.vector.tensor_copy(
+                gw[:, i * half : (i + 1) * half], xw[:].indirect(offs_sb[:, i * half // 16 : (i + 1) * half // 16])
+            )
+
+        deal(w1s_d[:], w1s[:])
+
+        def first_product(acc, t, cols):
+            w_cols = slice(t * P, (t + 1) * P)
+            nc.tensor.matmul_mx(
+                out=acc,
+                lhsT=w1w_d[:, w_cols].bitcast(FP8X4),
+                lhsT_scale=w1s_d[W1_ROW:, w_cols],
+                rhs=gw[:, cols].bitcast(FP8X4),
+                rhs_scale=gs[:, cols],
+                start=True,
+                stop=True,
+            )
+
+        pre = [keep.tile([P, S], F32, name=f"pre{t}", align_bytes=64) for t in range(PACK)]
+        for i in range(2):
+            cols = slice(i * half, (i + 1) * half)
+            acc = psum.tile([P, half], F32, name=f"acc0_{i}")
+            first_product(acc[:], 0, cols)
+            nc.scalar.copy(pre[0][:, cols], acc[:])
+        for t in range(1, PACK):
+            acc = psum.tile([P, S], F32, name=f"acc{t}")
+            first_product(acc[:], t, slice(0, S))
+            nc.vector.tensor_copy(pre[t][:], acc[:])
+
+        deal(w2w_d[:].bitcast(I32), w2w[:].bitcast(I32))
+        deal(w2s_d[:], w2s[:])
+
+        z_words = keep.tile([P, S], U32, align_bytes=64)
+        z_scales = keep.tile([P, S], U8, align_bytes=64)
+        y_words = keep.tile([P, S], U32, align_bytes=64)
+        y_scales = keep.tile([P, S], U8, align_bytes=64)
+        out_rows = out_0.rearrange("(p t) j -> p t j", t=PACK)
+        out_words = as_words(out_1)
+
+        def fetch(dst, t, places, j0, n, scale):
+            nc.scalar.activation(
+                dst[:, t, :], pre[t][:].indirect(places[:, j0 // 16 : (j0 + n) // 16]), ACT.Sigmoid, scale=scale
+            )
+
+        def logic(j0, n):
+            not_a = keep.tile([P, PACK, n], F32, name=f"not_a{j0}", align_bytes=64)
+            b = keep.tile([P, PACK, n], F32, name=f"b{j0}", align_bytes=64)
+            c = keep.tile([P, PACK, n], F32, name=f"c{j0}", align_bytes=64)
+            conj = keep.tile([P, PACK, n], F32, name=f"conj{j0}", align_bytes=64)
+            impl = keep.tile([P, PACK, n], F32, name=f"impl{j0}", align_bytes=64)
+            larger = keep.tile([P, PACK, n], F32, name=f"larger{j0}", align_bytes=64)
+            z = keep.tile([P, n, PACK], BF16, name=f"z{j0}", align_bytes=64)
+            for t0 in (0, 2):
+                pair = slice(t0, t0 + 2)
+                for dst, places, scale in ((not_a, c1_sb, -2.0), (c, c3_sb, 2.0), (b, c2_sb, 2.0)):
+                    for t in (t0, t0 + 1):
+                        fetch(dst, t, places, j0, n, scale)
+                nc.vector.tensor_tensor(conj[:, pair, :], c[:, pair, :], not_a[:, pair, :], ALU.subtract)
+                nc.vector.scalar_tensor_tensor(
+                    impl[:, pair, :], b[:, pair, :], 0.5, not_a[:, pair, :], ALU.subtract, ALU.add
+                )
+                nc.vector.scalar_tensor_tensor(
+                    larger[:, pair, :], impl[:, pair, :], 0.5, conj[:, pair, :], ALU.min, ALU.max
+                )
+            nc.vector.scalar_tensor_tensor(
+                z[:],
+                larger[:].rearrange("p t j -> p j t"),
+                0.0,
+                gain[:].unsqueeze(1).to_broadcast([P, n, PACK]),
+                ALU.max,
+                ALU.mult,
+            )
+            cols = slice(j0, j0 + n)
+            nc.vector.quantize_mx(
+                out=z_words[:, cols].bitcast(FP8X4), scales=z_scales[:, cols], in_=z[:].rearrange("p j t -> p (j t)")
+            )
+
+        def second_product(j0):
+            cols = slice(j0, j0 + BLOCK)
+            acc = psum.tile([P, PACK, BLOCK], F32, name="acc_out", bufs=3)
+            for t in range(PACK):
+                w_cols = slice(t * P, (t + 1) * P)
+                nc.tensor.matmul_mx(
+                    out=acc[:, t, :],
+                    lhsT=w2w_d[:, w_cols].bitcast(FP8X4),
+                    lhsT_scale=w2s_d[W2_ROW:, w_cols],
+                    rhs=z_words[:, cols].bitcast(FP8X4),
+                    rhs_scale=z_scales[:, cols],
+                    start=True,
+                    stop=True,
+                )
+            return acc
+
+        def hand_out(j0, acc, scalar_free):
+            cols = slice(j0, j0 + BLOCK)
+            y = keep.tile([P, PACK, BLOCK], F32, name=f"y{j0}", align_bytes=64)
+            y16 = keep.tile([P, BLOCK, PACK], BF16, name=f"y16_{j0}", align_bytes=64)
+            if scalar_free:
+                nc.vector.tensor_copy(y16[:], acc[:].rearrange("p t j -> p j t"))
+                nc.scalar.copy(y[:], acc[:])
+            else:
+                nc.vector.tensor_copy(y[:], acc[:])
+                nc.vector.tensor_copy(y16[:], y[:].rearrange("p t j -> p j t"))
+            nc.vector.quantize_mx(
+                out=y_words[:, cols].bitcast(FP8X4), scales=y_scales[:, cols], in_=y16[:].rearrange("p j t -> p (j t)")
+            )
+            nc.sync.dma_start(out=out_rows[:, :, cols], in_=y[:])
+            nc.sync.dma_start(out=out_words[:, cols], in_=y_words[:, cols].bitcast(I32))
+
+        waiting = []
+        for j0, n in CHUNKS:
+            logic(j0, n)
+            for args in waiting:
+                hand_out(*args)
+            waiting = [(j, second_product(j), j >= 256) for j in range(j0, j0 + n, BLOCK)]
+        for args in waiting:
+            hand_out(*args)
+        for q in range(QUADS):
+            queue = nc.sync if q % 2 == 0 else nc.scalar
+            queue.dma_start(
+                out=out_2[0, 4 * q : 4 * q + 4, :].bitcast(I32), in_=y_scales[32 * q : 32 * q + 4, :].bitcast(I32)
+            )

@@ -60,18 +60,18 @@ def tile_picked_lukaslog_none_po_kernel(
         warm = keep.tile([P, 2], F32, align_bytes=64)
 
         nc.vector.memset(xs[:].bitcast(I32), 0)
-        nc.gpsimd.memset(w1s[:].bitcast(I32), 0)
+        nc.vector.memset(w1s[:].bitcast(I32), 0)
         nc.vector.memset(w2s[:].bitcast(I32), 0)
         nc.vector.memset(warm[:, 0:1], 0.0)
         nc.scalar.activation(warm[:, 1:2], warm[:, 0:1], ACT.Sigmoid)
 
         nc.sync.dma_start(offs_sb[:], offs)
         nc.sync.dma_start(out=w1w[:].bitcast(I32), in_=as_words(w1_words))
-        nc.sync.dma_start(out=xw[:].bitcast(I32), in_=as_words(x_words))
         for q in range(QUADS):
             load_scale_rows(nc.sync, xs, x_scales, 0, q)
+        nc.sync.dma_start(out=xw[:].bitcast(I32), in_=as_words(x_words))
         for q in range(QUADS):
-            load_scale_rows(nc.gpsimd if q == 3 else nc.sync, w1s, w1_scales, W1_ROW, q)
+            load_scale_rows(nc.sync, w1s, w1_scales, W1_ROW, q)
         nc.sync.dma_start(c1_sb[:], c1)
         nc.sync.dma_start(c3_sb[:], c3)
         nc.sync.dma_start(c2_sb[:], c2)
@@ -95,7 +95,9 @@ def tile_picked_lukaslog_none_po_kernel(
                 gw[:, i * half : (i + 1) * half], xw[:].indirect(offs_sb[:, i * half // 16 : (i + 1) * half // 16])
             )
 
-        deal(w1s_d[:], w1s[:])
+        w1s_by_tile = w1s[:].rearrange("p (m t) -> p t m", t=PACK)
+        nc.vector.tensor_copy(w1s_d[:, :P], w1s_by_tile[:, 0, :])
+        nc.vector.tensor_copy(w1s_d[:, P:].rearrange("p (t m) -> p t m", m=P), w1s_by_tile[:, 1:, :])
 
         def first_product(acc, t, cols):
             w_cols = slice(t * P, (t + 1) * P)
@@ -109,68 +111,105 @@ def tile_picked_lukaslog_none_po_kernel(
                 stop=True,
             )
 
-        pre = [keep.tile([P, S], F32, name=f"pre{t}", align_bytes=64) for t in range(PACK)]
+        pre = {t: keep.tile([P, S], F32, name=f"pre{t}", align_bytes=64) for t in range(1, PACK)}
+        truth = keep.tile([P, S], F32, align_bytes=64)
+        truth_less_half = keep.tile([P, S], F32, align_bytes=64)
         for i in range(2):
             cols = slice(i * half, (i + 1) * half)
-            acc = psum.tile([P, half], F32, name=f"acc0_{i}")
+            acc = psum.tile([P, half], F32, name="bank", bufs=8)
             first_product(acc[:], 0, cols)
-            nc.scalar.copy(pre[0][:, cols], acc[:])
+            nc.scalar.activation(truth[:, cols], acc[:], ACT.Sigmoid, scale=2.0)
+        first_sums = {}
         for t in range(1, PACK):
-            acc = psum.tile([P, S], F32, name=f"acc{t}")
-            first_product(acc[:], t, slice(0, S))
-            nc.vector.tensor_copy(pre[t][:], acc[:])
-
-        deal(w2w_d[:].bitcast(I32), w2w[:].bitcast(I32))
-        deal(w2s_d[:], w2s[:])
+            first_sums[t] = psum.tile([P, S], F32, name="bank", bufs=8)
+            first_product(first_sums[t][:], t, slice(0, S))
+        nc.scalar.copy(pre[1][:], first_sums[1][:])
 
         z_words = keep.tile([P, S], U32, align_bytes=64)
         z_scales = keep.tile([P, S], U8, align_bytes=64)
         y_words = keep.tile([P, S], U32, align_bytes=64)
         y_scales = keep.tile([P, S], U8, align_bytes=64)
+        conj0 = keep.tile([P, S], F32, align_bytes=64)
+        impl0 = keep.tile([P, S], F32, align_bytes=64)
+        larger = keep.tile([P, PACK, S], F32, align_bytes=64)
+        half_less_a = keep.tile([P, S], F32, align_bytes=64)
         out_rows = out_0.rearrange("(p t) j -> p t j", t=PACK)
         out_words = as_words(out_1)
 
-        def fetch(dst, t, places, j0, n, scale):
-            nc.scalar.activation(
-                dst[:, t, :], pre[t][:].indirect(places[:, j0 // 16 : (j0 + n) // 16]), ACT.Sigmoid, scale=scale
-            )
+        def entries(places, cols):
+            return places[:, cols.start // 16 : cols.stop // 16]
 
-        def logic(j0, n):
+        def vector_fetches(cols):
+            return [
+                lambda: nc.vector.tensor_scalar(
+                    half_less_a[:, cols], truth[:].indirect(entries(c1_sb, cols)), -1.0, 0.5, ALU.mult, ALU.add
+                ),
+                lambda: nc.vector.tensor_tensor(
+                    impl0[:, cols], truth[:].indirect(entries(c2_sb, cols)), half_less_a[:, cols], ALU.add
+                ),
+                lambda: nc.vector.tensor_tensor(
+                    conj0[:, cols],
+                    truth_less_half[:].indirect(entries(c3_sb, cols)),
+                    half_less_a[:, cols],
+                    ALU.subtract,
+                ),
+                lambda: nc.vector.scalar_tensor_tensor(
+                    larger[:, 0, cols], impl0[:, cols], 0.5, conj0[:, cols], ALU.min, ALU.max
+                ),
+            ]
+
+        def logic(j0, n, groups, fillers):
+            cols = slice(j0, j0 + n)
             not_a = keep.tile([P, PACK, n], F32, name=f"not_a{j0}", align_bytes=64)
             b = keep.tile([P, PACK, n], F32, name=f"b{j0}", align_bytes=64)
             c = keep.tile([P, PACK, n], F32, name=f"c{j0}", align_bytes=64)
-            conj = keep.tile([P, PACK, n], F32, name=f"conj{j0}", align_bytes=64)
-            impl = keep.tile([P, PACK, n], F32, name=f"impl{j0}", align_bytes=64)
-            larger = keep.tile([P, PACK, n], F32, name=f"larger{j0}", align_bytes=64)
-            z = keep.tile([P, n, PACK], BF16, name=f"z{j0}", align_bytes=64)
-            for t0 in (0, 2):
-                pair = slice(t0, t0 + 2)
-                for dst, places, scale in ((not_a, c1_sb, -2.0), (c, c3_sb, 2.0), (b, c2_sb, 2.0)):
-                    for t in (t0, t0 + 1):
-                        fetch(dst, t, places, j0, n, scale)
-                nc.vector.tensor_tensor(conj[:, pair, :], c[:, pair, :], not_a[:, pair, :], ALU.subtract)
-                nc.vector.scalar_tensor_tensor(
-                    impl[:, pair, :], b[:, pair, :], 0.5, not_a[:, pair, :], ALU.subtract, ALU.add
+            conj = keep.tile([P, PACK, n], F32, name="conj", align_bytes=64)
+            impl = keep.tile([P, PACK, n], F32, name="impl", align_bytes=64)
+            z = keep.tile([P, n, PACK], BF16, name="rounded", align_bytes=64)
+            fetches = ((not_a, c1_sb, -2.0), (c, c3_sb, 2.0), (b, c2_sb, 2.0))
+            tiles = range(1, PACK)
+            if j0 == 0:
+                order = [(t, f) for t in tiles for f in fetches]
+            else:
+                order = [(t, f) for f in fetches for t in tiles]
+            for t, (dst, places, scale) in order:
+                nc.scalar.activation(dst[:, t, :], pre[t][:].indirect(entries(places, cols)), ACT.Sigmoid, scale=scale)
+
+            def implication(ts):
+                nc.vector.scalar_tensor_tensor(impl[:, ts, :], b[:, ts, :], 0.5, not_a[:, ts, :], ALU.subtract, ALU.add)
+
+            def take_larger(ts):
+                nc.vector.scalar_tensor_tensor(larger[:, ts, cols], impl[:, ts, :], 0.5, conj[:, ts, :], ALU.min, ALU.max)
+
+            steps = [lambda: nc.vector.tensor_tensor(conj[:, 1:, :], c[:, 1:, :], not_a[:, 1:, :], ALU.subtract)]
+            for t0, t1 in groups:
+                steps.append(lambda t0=t0, t1=t1: implication(slice(t0, t1)))
+                steps.append(lambda t0=t0, t1=t1: take_larger(slice(t0, t1)))
+            steps.append(
+                lambda: nc.vector.scalar_tensor_tensor(
+                    z[:],
+                    larger[:, :, cols].rearrange("p t j -> p j t"),
+                    0.0,
+                    gain[:].unsqueeze(1).to_broadcast([P, n, PACK]),
+                    ALU.max,
+                    ALU.mult,
                 )
-                nc.vector.scalar_tensor_tensor(
-                    larger[:, pair, :], impl[:, pair, :], 0.5, conj[:, pair, :], ALU.min, ALU.max
+            )
+            steps.append(
+                lambda: nc.vector.quantize_mx(
+                    out=z_words[:, cols].bitcast(FP8X4),
+                    scales=z_scales[:, cols],
+                    in_=z[:].rearrange("p j t -> p (j t)"),
                 )
-            nc.vector.scalar_tensor_tensor(
-                z[:],
-                larger[:].rearrange("p t j -> p j t"),
-                0.0,
-                gain[:].unsqueeze(1).to_broadcast([P, n, PACK]),
-                ALU.max,
-                ALU.mult,
             )
-            cols = slice(j0, j0 + n)
-            nc.vector.quantize_mx(
-                out=z_words[:, cols].bitcast(FP8X4), scales=z_scales[:, cols], in_=z[:].rearrange("p j t -> p (j t)")
-            )
+            for i, step in enumerate(steps):
+                step()
+                if 1 <= i <= len(fillers):
+                    fillers[i - 1]()
 
         def second_product(j0):
             cols = slice(j0, j0 + BLOCK)
-            acc = psum.tile([P, PACK, BLOCK], F32, name="acc_out", bufs=3)
+            acc = psum.tile([P, PACK, BLOCK], F32, name="bank", bufs=8)
             for t in range(PACK):
                 w_cols = slice(t * P, (t + 1) * P)
                 nc.tensor.matmul_mx(
@@ -184,30 +223,53 @@ def tile_picked_lukaslog_none_po_kernel(
                 )
             return acc
 
-        def hand_out(j0, acc, scalar_free):
-            cols = slice(j0, j0 + BLOCK)
-            y = keep.tile([P, PACK, BLOCK], F32, name=f"y{j0}", align_bytes=64)
-            y16 = keep.tile([P, BLOCK, PACK], BF16, name=f"y16_{j0}", align_bytes=64)
-            if scalar_free:
-                nc.vector.tensor_copy(y16[:], acc[:].rearrange("p t j -> p j t"))
-                nc.scalar.copy(y[:], acc[:])
-            else:
-                nc.vector.tensor_copy(y[:], acc[:])
-                nc.vector.tensor_copy(y16[:], y[:].rearrange("p t j -> p j t"))
+        deal(w2w_d[:].bitcast(I32), w2w[:].bitcast(I32))
+        early = vector_fetches(slice(0, half))
+        later = vector_fetches(slice(half, S))
+        early[0]()
+        nc.vector.tensor_copy(pre[2][:], first_sums[2][:])
+        nc.vector.tensor_scalar(truth_less_half[:], truth[:], 0.5, None, ALU.subtract)
+        nc.scalar.copy(pre[3][:], first_sums[3][:])
+        early[1]()
+        early[2]()
+        later[0]()
+        early[3]()
+        fillers = [[lambda: deal(w2s_d[:], w2s[:]), later[1], later[2], later[3]], [], []]
+        sums = []
+        for (j0, n), fill in zip(CHUNKS, fillers):
+            last = j0 + n == S
+            logic(j0, n, ((1, 3), (3, 4)) if last else ((1, 4),), fill)
+            for j in range(j0, j0 + n, BLOCK):
+                sums.append(second_product(j))
+
+        y = keep.tile([P, PACK, S], F32, align_bytes=64)
+        y16 = keep.tile([P, S, PACK], BF16, name="rounded", align_bytes=64)
+
+        def store_sums(cols, acc):
+            nc.scalar.copy(y[:, :, cols], acc[:])
+            nc.sync.dma_start(out=out_rows[:, :, cols], in_=y[:, :, cols])
+
+        def round_sums(cols):
+            nc.vector.tensor_copy(y16[:, cols, :], y[:, :, cols].rearrange("p t j -> p j t"))
+
+        def planes(cols):
             nc.vector.quantize_mx(
-                out=y_words[:, cols].bitcast(FP8X4), scales=y_scales[:, cols], in_=y16[:].rearrange("p j t -> p (j t)")
+                out=y_words[:, cols].bitcast(FP8X4),
+                scales=y_scales[:, cols],
+                in_=y16[:, cols, :].rearrange("p j t -> p (j t)"),
             )
-            nc.sync.dma_start(out=out_rows[:, :, cols], in_=y[:])
             nc.sync.dma_start(out=out_words[:, cols], in_=y_words[:, cols].bitcast(I32))
 
-        waiting = []
-        for j0, n in CHUNKS:
-            logic(j0, n)
-            for args in waiting:
-                hand_out(*args)
-            waiting = [(j, second_product(j), j >= 256) for j in range(j0, j0 + n, BLOCK)]
-        for args in waiting:
-            hand_out(*args)
+        blocks = [slice(j, j + BLOCK) for j in range(0, S, BLOCK)]
+        for cols, acc in zip(blocks[:-1], sums):
+            store_sums(cols, acc)
+        nc.scalar.copy(y16[:, blocks[0], :], sums[0][:].rearrange("p t j -> p j t"))
+        round_sums(slice(BLOCK, S - BLOCK))
+        planes(slice(0, half))
+        planes(blocks[-2])
+        store_sums(blocks[-1], sums[-1])
+        round_sums(blocks[-1])
+        planes(blocks[-1])
         for q in range(QUADS):
             queue = nc.sync if q % 2 == 0 else nc.scalar
             queue.dma_start(

@@ -35,10 +35,14 @@ def tile_picked_lukaslog_none_po_kernel(
         rows = slice(32 * q + first_row, 32 * q + first_row + 4)
         queue.dma_start(out=tile[rows, :].bitcast(I32), in_=dram[0, 4 * q : 4 * q + 4, :].bitcast(I32))
 
-    def deal(dealt, raw):
+    def deal(dealt, raw, run):
         nc.vector.tensor_copy(
-            out=dealt.rearrange("p (t m) -> p t m", t=PACK), in_=raw.rearrange("p (m t) -> p t m", t=PACK)
+            out=dealt.rearrange("p (t c i) -> p c t i", t=PACK, i=run),
+            in_=raw.rearrange("p (c i t) -> p c t i", t=PACK, i=run),
         )
+
+    def weave(copy, woven, rows):
+        copy(woven.rearrange("p (c i) t -> p c t i", i=4), rows.rearrange("p t (c i) -> p c t i", i=4))
 
     with ExitStack() as ctx:
         lists = ctx.enter_context(tc.tile_pool(name="lists", bufs=1))
@@ -87,7 +91,7 @@ def tile_picked_lukaslog_none_po_kernel(
         gw = keep.tile([P, S], U32, align_bytes=64)
         gs = keep.tile([P, S], U8, align_bytes=64)
 
-        deal(w1w_d[:].bitcast(I32), w1w[:].bitcast(I32))
+        deal(w1w_d[:].bitcast(I32), w1w[:].bitcast(I32), 4)
         nc.vector.tensor_copy(gs[:], xs[:].indirect(offs_sb[:]))
         half = S // 2
         for i in range(2):
@@ -132,6 +136,11 @@ def tile_picked_lukaslog_none_po_kernel(
         conj0 = keep.tile([P, S], F32, align_bytes=64)
         impl0 = keep.tile([P, S], F32, align_bytes=64)
         larger = keep.tile([P, PACK, S], F32, align_bytes=64)
+        z_rows = keep.tile([P, PACK, S], BF16, align_bytes=64)
+
+        def apply_gain(t, cols):
+            nc.vector.tensor_scalar(z_rows[:, t, cols], larger[:, t, cols], 0.0, gain[:, t : t + 1], ALU.max, ALU.mult)
+
         half_less_a = keep.tile([P, S], F32, align_bytes=64)
         out_rows = out_0.rearrange("(p t) j -> p t j", t=PACK)
         out_words = as_words(out_1)
@@ -156,6 +165,7 @@ def tile_picked_lukaslog_none_po_kernel(
                 lambda: nc.vector.scalar_tensor_tensor(
                     larger[:, 0, cols], impl0[:, cols], 0.5, conj0[:, cols], ALU.min, ALU.max
                 ),
+                lambda: apply_gain(0, cols),
             ]
 
         def logic(j0, n, groups, fillers):
@@ -185,16 +195,9 @@ def tile_picked_lukaslog_none_po_kernel(
             for t0, t1 in groups:
                 steps.append(lambda t0=t0, t1=t1: implication(slice(t0, t1)))
                 steps.append(lambda t0=t0, t1=t1: take_larger(slice(t0, t1)))
-            steps.append(
-                lambda: nc.vector.scalar_tensor_tensor(
-                    z[:],
-                    larger[:, :, cols].rearrange("p t j -> p j t"),
-                    0.0,
-                    gain[:].unsqueeze(1).to_broadcast([P, n, PACK]),
-                    ALU.max,
-                    ALU.mult,
-                )
-            )
+                for t in range(t0, t1):
+                    steps.append(lambda t=t: apply_gain(t, cols))
+            steps.append(lambda: weave(nc.vector.tensor_copy, z[:], z_rows[:, :, cols]))
             steps.append(
                 lambda: nc.vector.quantize_mx(
                     out=z_words[:, cols].bitcast(FP8X4),
@@ -223,18 +226,19 @@ def tile_picked_lukaslog_none_po_kernel(
                 )
             return acc
 
-        deal(w2w_d[:].bitcast(I32), w2w[:].bitcast(I32))
+        deal(w2w_d[:].bitcast(I32), w2w[:].bitcast(I32), 4)
         early = vector_fetches(slice(0, half))
         later = vector_fetches(slice(half, S))
         early[0]()
         nc.vector.tensor_copy(pre[2][:], first_sums[2][:])
         nc.vector.tensor_scalar(truth_less_half[:], truth[:], 0.5, None, ALU.subtract)
-        nc.scalar.copy(pre[3][:], first_sums[3][:])
+        nc.vector.tensor_copy(pre[3][:], first_sums[3][:])
         early[1]()
         early[2]()
         later[0]()
         early[3]()
-        fillers = [[lambda: deal(w2s_d[:], w2s[:]), later[1], later[2], later[3]], [], []]
+        early[4]()
+        fillers = [[lambda: deal(w2s_d[:], w2s[:], 16), *later[1:]], [], []]
         sums = []
         for (j0, n), fill in zip(CHUNKS, fillers):
             last = j0 + n == S
@@ -250,7 +254,7 @@ def tile_picked_lukaslog_none_po_kernel(
             nc.sync.dma_start(out=out_rows[:, :, cols], in_=y[:, :, cols])
 
         def round_sums(cols):
-            nc.vector.tensor_copy(y16[:, cols, :], y[:, :, cols].rearrange("p t j -> p j t"))
+            weave(nc.vector.tensor_copy, y16[:, cols, :], y[:, :, cols])
 
         def planes(cols):
             nc.vector.quantize_mx(
@@ -263,7 +267,7 @@ def tile_picked_lukaslog_none_po_kernel(
         blocks = [slice(j, j + BLOCK) for j in range(0, S, BLOCK)]
         for cols, acc in zip(blocks[:-1], sums):
             store_sums(cols, acc)
-        nc.scalar.copy(y16[:, blocks[0], :], sums[0][:].rearrange("p t j -> p j t"))
+        weave(nc.scalar.copy, y16[:, blocks[0], :], sums[0][:])
         round_sums(slice(BLOCK, S - BLOCK))
         planes(slice(0, half))
         planes(blocks[-2])

@@ -61,13 +61,10 @@ def tile_picked_lukaslog_none_po_kernel(
         w2w = keep.tile([P, N], U32, align_bytes=64)
         w2s = keep.tile([P, N], U8, align_bytes=64)
         gain = keep.tile([P, PACK], F32, align_bytes=64)
-        warm = keep.tile([P, 2], F32, align_bytes=64)
 
         nc.vector.memset(xs[:].bitcast(I32), 0)
         nc.vector.memset(w1s[:].bitcast(I32), 0)
         nc.vector.memset(w2s[:].bitcast(I32), 0)
-        nc.vector.memset(warm[:, 0:1], 0.0)
-        nc.scalar.activation(warm[:, 1:2], warm[:, 0:1], ACT.Sigmoid)
 
         nc.sync.dma_start(offs_sb[:], offs)
         nc.sync.dma_start(out=w1w[:].bitcast(I32), in_=as_words(w1_words))
@@ -249,31 +246,37 @@ def tile_picked_lukaslog_none_po_kernel(
         y = keep.tile([P, PACK, S], F32, align_bytes=64)
         y16 = keep.tile([P, S, PACK], BF16, name="rounded", align_bytes=64)
 
-        def store_sums(cols, acc):
-            nc.scalar.copy(y[:, :, cols], acc[:])
+        def store_sums(cols):
             nc.sync.dma_start(out=out_rows[:, :, cols], in_=y[:, :, cols])
 
         def round_sums(cols):
             weave(nc.vector.tensor_copy, y16[:, cols, :], y[:, :, cols])
 
-        def planes(cols):
+        def quantise_sums(cols):
             nc.vector.quantize_mx(
                 out=y_words[:, cols].bitcast(FP8X4),
                 scales=y_scales[:, cols],
                 in_=y16[:, cols, :].rearrange("p j t -> p (j t)"),
             )
+
+        def store_words(cols):
             nc.sync.dma_start(out=out_words[:, cols], in_=y_words[:, cols].bitcast(I32))
 
         blocks = [slice(j, j + BLOCK) for j in range(0, S, BLOCK)]
         for cols, acc in zip(blocks[:-1], sums):
-            store_sums(cols, acc)
+            nc.scalar.copy(y[:, :, cols], acc[:])
+        store_sums(slice(0, half))
+        store_sums(blocks[-2])
         weave(nc.scalar.copy, y16[:, blocks[0], :], sums[0][:])
         round_sums(slice(BLOCK, S - BLOCK))
-        planes(slice(0, half))
-        planes(blocks[-2])
-        store_sums(blocks[-1], sums[-1])
+        quantise_sums(slice(0, half))
+        quantise_sums(blocks[-2])
+        store_words(slice(0, S - BLOCK))
+        nc.scalar.copy(y[:, :, blocks[-1]], sums[-1][:])
+        store_sums(blocks[-1])
         round_sums(blocks[-1])
-        planes(blocks[-1])
+        quantise_sums(blocks[-1])
+        store_words(blocks[-1])
         for q in range(QUADS):
             queue = nc.sync if q % 2 == 0 else nc.scalar
             queue.dma_start(

from contextlib import ExitStack

import concourse.mybir as mybir

K, T, S, H, N = 512, 2048, 512, 512, 512
FLOPS = 2 * K * H * S + 2 * H * N * S

F32 = mybir.dt.float32
BF16 = mybir.dt.bfloat16
I32 = mybir.dt.int32
U32 = mybir.dt.uint32
U16 = mybir.dt.uint16
U8 = mybir.dt.uint8
FP8X4 = mybir.dt.float8_e4m3fn_x4
ALU = mybir.AluOpType
ACT = mybir.ActivationFunctionType

P = 128
PACK = 4
QUADS = 4
BLOCK = 128
CHUNKS = ((0, 256), (256, 128), (384, 128))
W1_ROW, W2_ROW = 4, 8


def tile_picked_lukaslog_none_po_kernel(
    tc, x_words, x_scales, w1_words, w1_scales, gn, w2_words, w2_scales, offs, c1, c2, c3, out_0, out_1, out_2
):
    nc = tc.nc

    def as_words(dram):
        return dram[0].rearrange("p n t -> p (n t)").bitcast(I32)

    def load_scale_rows(queue, tile, dram, first_row, q):
        rows = slice(32 * q + first_row, 32 * q + first_row + 4)
        queue.dma_start(out=tile[rows, :].bitcast(I32), in_=dram[0, 4 * q : 4 * q + 4, :].bitcast(I32))

    def deal(dealt, raw, run):
        nc.vector.tensor_copy(
            out=dealt.rearrange("p (t c i) -> p c t i", t=PACK, i=run),
            in_=raw.rearrange("p (c i t) -> p c t i", t=PACK, i=run),
        )

    def weave(copy, woven, rows):
        copy(woven.rearrange("p (c i) t -> p c t i", i=4), rows.rearrange("p t (c i) -> p c t i", i=4))

    with ExitStack() as ctx:
        lists = ctx.enter_context(tc.tile_pool(name="lists", bufs=1))
        keep = ctx.enter_context(tc.tile_pool(name="keep", bufs=1))
        psum = ctx.enter_context(tc.psum_pool(name="psum", bufs=1))

        offs_sb = lists.tile([P, S // 16], U16)
        c1_sb = lists.tile([P, S // 16], U16)
        c2_sb = lists.tile([P, S // 16], U16)
        c3_sb = lists.tile([P, S // 16], U16)

        xw = keep.tile([P, T], U32, align_bytes=64)
        xs = keep.tile([P, T], U8, align_bytes=64)
        w1w = keep.tile([P, H], U32, align_bytes=64)
        w1s = keep.tile([P, H], U8, align_bytes=64)
        w2w = keep.tile([P, N], U32, align_bytes=64)
        w2s = keep.tile([P, N], U8, align_bytes=64)
        gain = keep.tile([P, PACK], F32, align_bytes=64)

        nc.vector.memset(xs[:].bitcast(I32), 0)
        nc.vector.memset(w1s[:].bitcast(I32), 0)
        nc.vector.memset(w2s[:].bitcast(I32), 0)

        nc.sync.dma_start(offs_sb[:], offs)
        nc.sync.dma_start(out=w1w[:].bitcast(I32), in_=as_words(w1_words))
        for q in range(QUADS):
            load_scale_rows(nc.sync, xs, x_scales, 0, q)
        nc.sync.dma_start(out=xw[:].bitcast(I32), in_=as_words(x_words))
        for q in range(QUADS):
            load_scale_rows(nc.sync, w1s, w1_scales, W1_ROW, q)
        nc.sync.dma_start(c1_sb[:], c1)
        nc.sync.dma_start(c3_sb[:], c3)
        nc.sync.dma_start(c2_sb[:], c2)
        nc.sync.dma_start(out=gain[:], in_=gn.rearrange("(p t) o -> p (t o)", t=PACK))
        nc.sync.dma_start(out=w2w[:].bitcast(I32), in_=as_words(w2_words))
        for q in range(QUADS):
            load_scale_rows(nc.sync, w2s, w2_scales, W2_ROW, q)

        w1w_d = keep.tile([P, H], U32, align_bytes=64)
        w1s_d = keep.tile([P, H], U8, align_bytes=64)
        w2w_d = keep.tile([P, N], U32, align_bytes=64)
        w2s_d = keep.tile([P, N], U8, align_bytes=64)
        gw = keep.tile([P, S], U32, align_bytes=64)
        gs = keep.tile([P, S], U8, align_bytes=64)

        deal(w1w_d[:].bitcast(I32), w1w[:].bitcast(I32), 4)
        nc.vector.tensor_copy(gs[:], xs[:].indirect(offs_sb[:]))
        half = S // 2
        for i in range(2):
            nc.vector.tensor_copy(
                gw[:, i * half : (i + 1) * half], xw[:].indirect(offs_sb[:, i * half // 16 : (i + 1) * half // 16])
            )

        w1s_by_tile = w1s[:].rearrange("p (m t) -> p t m", t=PACK)
        nc.vector.tensor_copy(w1s_d[:, :P], w1s_by_tile[:, 0, :])
        nc.vector.tensor_copy(w1s_d[:, P:].rearrange("p (t m) -> p t m", m=P), w1s_by_tile[:, 1:, :])

        def first_product(acc, t, cols):
            w_cols = slice(t * P, (t + 1) * P)
            nc.tensor.matmul_mx(
                out=acc,
                lhsT=w1w_d[:, w_cols].bitcast(FP8X4),
                lhsT_scale=w1s_d[W1_ROW:, w_cols],
                rhs=gw[:, cols].bitcast(FP8X4),
                rhs_scale=gs[:, cols],
                start=True,
                stop=True,
            )

        pre = {t: keep.tile([P, S], F32, name=f"pre{t}", align_bytes=64) for t in range(1, PACK)}
        truth = keep.tile([P, S], F32, align_bytes=64)
        truth_less_half = keep.tile([P, S], F32, align_bytes=64)
        for i in range(2):
            cols = slice(i * half, (i + 1) * half)
            acc = psum.tile([P, half], F32, name="bank", bufs=8)
            first_product(acc[:], 0, cols)
            nc.scalar.activation(truth[:, cols], acc[:], ACT.Sigmoid, scale=2.0)
        first_sums = {}
        for t in range(1, PACK):
            first_sums[t] = psum.tile([P, S], F32, name="bank", bufs=8)
            first_product(first_sums[t][:], t, slice(0, S))
        nc.scalar.copy(pre[1][:], first_sums[1][:])

        z_words = keep.tile([P, S], U32, align_bytes=64)
        z_scales = keep.tile([P, S], U8, align_bytes=64)
        y_words = keep.tile([P, S], U32, align_bytes=64)
        y_scales = keep.tile([P, S], U8, align_bytes=64)
        conj0 = keep.tile([P, S], F32, align_bytes=64)
        impl0 = keep.tile([P, S], F32, align_bytes=64)
        larger = keep.tile([P, PACK, S], F32, align_bytes=64)
        z_rows = keep.tile([P, PACK, S], BF16, align_bytes=64)

        def apply_gain(t, cols):
            nc.vector.tensor_scalar(z_rows[:, t, cols], larger[:, t, cols], 0.0, gain[:, t : t + 1], ALU.max, ALU.mult)

        half_less_a = keep.tile([P, S], F32, align_bytes=64)
        out_rows = out_0.rearrange("(p t) j -> p t j", t=PACK)
        out_words = as_words(out_1)

        def entries(places, cols):
            return places[:, cols.start // 16 : cols.stop // 16]

        def vector_fetches(cols):
            return [
                lambda: nc.vector.tensor_scalar(
                    half_less_a[:, cols], truth[:].indirect(entries(c1_sb, cols)), -1.0, 0.5, ALU.mult, ALU.add
                ),
                lambda: nc.vector.tensor_tensor(
                    impl0[:, cols], truth[:].indirect(entries(c2_sb, cols)), half_less_a[:, cols], ALU.add
                ),
                lambda: nc.vector.tensor_tensor(
                    conj0[:, cols],
                    truth_less_half[:].indirect(entries(c3_sb, cols)),
                    half_less_a[:, cols],
                    ALU.subtract,
                ),
                lambda: nc.vector.scalar_tensor_tensor(
                    larger[:, 0, cols], impl0[:, cols], 0.5, conj0[:, cols], ALU.min, ALU.max
                ),
                lambda: apply_gain(0, cols),
            ]

        def logic(j0, n, groups, fillers):
            cols = slice(j0, j0 + n)
            not_a = keep.tile([P, PACK, n], F32, name=f"not_a{j0}", align_bytes=64)
            b = keep.tile([P, PACK, n], F32, name=f"b{j0}", align_bytes=64)
            c = keep.tile([P, PACK, n], F32, name=f"c{j0}", align_bytes=64)
            conj = keep.tile([P, PACK, n], F32, name="conj", align_bytes=64)
            impl = keep.tile([P, PACK, n], F32, name="impl", align_bytes=64)
            z = keep.tile([P, n, PACK], BF16, name="rounded", align_bytes=64)
            fetches = ((not_a, c1_sb, -2.0), (c, c3_sb, 2.0), (b, c2_sb, 2.0))
            tiles = range(1, PACK)
            if j0 == 0:
                order = [(t, f) for t in tiles for f in fetches]
            else:
                order = [(t, f) for f in fetches for t in tiles]
            for t, (dst, places, scale) in order:
                nc.scalar.activation(dst[:, t, :], pre[t][:].indirect(entries(places, cols)), ACT.Sigmoid, scale=scale)

            def implication(ts):
                nc.vector.scalar_tensor_tensor(impl[:, ts, :], b[:, ts, :], 0.5, not_a[:, ts, :], ALU.subtract, ALU.add)

            def take_larger(ts):
                nc.vector.scalar_tensor_tensor(larger[:, ts, cols], impl[:, ts, :], 0.5, conj[:, ts, :], ALU.min, ALU.max)

            steps = [lambda: nc.vector.tensor_tensor(conj[:, 1:, :], c[:, 1:, :], not_a[:, 1:, :], ALU.subtract)]
            for t0, t1 in groups:
                steps.append(lambda t0=t0, t1=t1: implication(slice(t0, t1)))
                steps.append(lambda t0=t0, t1=t1: take_larger(slice(t0, t1)))
                for t in range(t0, t1):
                    steps.append(lambda t=t: apply_gain(t, cols))
            steps.append(lambda: weave(nc.vector.tensor_copy, z[:], z_rows[:, :, cols]))
            steps.append(
                lambda: nc.vector.quantize_mx(
                    out=z_words[:, cols].bitcast(FP8X4),
                    scales=z_scales[:, cols],
                    in_=z[:].rearrange("p j t -> p (j t)"),
                )
            )
            for i, step in enumerate(steps):
                step()
                if 1 <= i <= len(fillers):
                    fillers[i - 1]()

        def second_product(j0):
            cols = slice(j0, j0 + BLOCK)
            acc = psum.tile([P, PACK, BLOCK], F32, name="bank", bufs=8)
            for t in range(PACK):
                w_cols = slice(t * P, (t + 1) * P)
                nc.tensor.matmul_mx(
                    out=acc[:, t, :],
                    lhsT=w2w_d[:, w_cols].bitcast(FP8X4),
                    lhsT_scale=w2s_d[W2_ROW:, w_cols],
                    rhs=z_words[:, cols].bitcast(FP8X4),
                    rhs_scale=z_scales[:, cols],
                    start=True,
                    stop=True,
                )
            return acc

        deal(w2w_d[:].bitcast(I32), w2w[:].bitcast(I32), 4)
        early = vector_fetches(slice(0, half))
        later = vector_fetches(slice(half, S))
        early[0]()
        nc.vector.tensor_copy(pre[2][:], first_sums[2][:])
        nc.vector.tensor_scalar(truth_less_half[:], truth[:], 0.5, None, ALU.subtract)
        nc.vector.tensor_copy(pre[3][:], first_sums[3][:])
        early[1]()
        early[2]()
        later[0]()
        early[3]()
        early[4]()
        fillers = [[lambda: deal(w2s_d[:], w2s[:], 16), *later[1:]], [], []]
        sums = []
        for (j0, n), fill in zip(CHUNKS, fillers):
            last = j0 + n == S
            logic(j0, n, ((1, 3), (3, 4)) if last else ((1, 4),), fill)
            for j in range(j0, j0 + n, BLOCK):
                sums.append(second_product(j))

        y = keep.tile([P, PACK, S], F32, align_bytes=64)
        y16 = keep.tile([P, S, PACK], BF16, name="rounded", align_bytes=64)

        def store_sums(cols):
            nc.sync.dma_start(out=out_rows[:, :, cols], in_=y[:, :, cols])

        def round_sums(cols):
            weave(nc.vector.tensor_copy, y16[:, cols, :], y[:, :, cols])

        def quantise_sums(cols):
            nc.vector.quantize_mx(
                out=y_words[:, cols].bitcast(FP8X4),
                scales=y_scales[:, cols],
                in_=y16[:, cols, :].rearrange("p j t -> p (j t)"),
            )

        def store_words(cols):
            nc.sync.dma_start(out=out_words[:, cols], in_=y_words[:, cols].bitcast(I32))

        blocks = [slice(j, j + BLOCK) for j in range(0, S, BLOCK)]
        for cols, acc in zip(blocks[:-1], sums):
            nc.scalar.copy(y[:, :, cols], acc[:])
        store_sums(slice(0, half))
        store_sums(blocks[-2])
        weave(nc.scalar.copy, y16[:, blocks[0], :], sums[0][:])
        round_sums(slice(BLOCK, S - BLOCK))
        quantise_sums(slice(0, half))
        quantise_sums(blocks[-2])
        store_words(slice(0, S - BLOCK))
        nc.scalar.copy(y[:, :, blocks[-1]], sums[-1][:])
        store_sums(blocks[-1])
        round_sums(blocks[-1])
        quantise_sums(blocks[-1])
        store_words(blocks[-1])
        for q in range(QUADS):
            queue = nc.sync if q % 2 == 0 else nc.scalar
            queue.dma_start(
                out=out_2[0, 4 * q : 4 * q + 4, :].bitcast(I32), in_=y_scales[32 * q : 32 * q + 4, :].bitcast(I32)
            )
